import numpy as np, ml_dtypes
CORES = [13,21,141,149]
N = 4
import mx_ref
NC, G = 384, 4
C = np.float32(0.019)
BF = ml_dtypes.bfloat16
def cut(t, i, w=512):
    return t[:, w * i:w * i + w]
def tile(rs):
    return np.stack(rs, axis=2).reshape(128, -1).astype(BF)
def layer(w, X):
    out = []
    for i in range(G):
        for t in range(len(X)):
            p = mx_ref.matmul(mx_ref.quantize(cut(w, len(X) * i + t)), X[t])
            z = p if t == 0 else z + p
        out.append(z)
    return out
def rot(Z, c, s):
    return [(Z[0] * c - Z[1] * s) * C, (Z[0] * s + Z[1] * c) * C, (Z[2] * c - Z[3] * s) * C, (Z[2] * s + Z[3] * c) * C]
def setup_inputs(rng):
    def f(*shape):
        return mx_ref.flush((rng.standard_normal(shape, dtype=np.float32) * np.exp2(rng.integers(-2, 3, shape[:-1] + (1,)))).astype(BF))
    ang = rng.random((N, 128, 128)) * (2 * np.pi)
    return {"cs": np.cos(ang).astype(BF), "sn": np.sin(ang).astype(BF), "xk": f(N, 128, 512), "wk": f(N, 128, G * 512), "xq": f(N, 128, 4 * NC)}
def setup_inputs_blocks(rng):
    d = setup_inputs(rng)
    for k in ("xk", "wk", "xq"): d[k] = mx_ref.spread(d[k], rng, 4)
    return d
def setup_inputs_wide(rng):
    d = setup_inputs(rng)
    for k in ("xk", "wk", "xq"): d[k] = mx_ref.flush((d[k].astype(np.float32) * np.exp2(rng.integers(-5, 6, (N, 1, 1))).astype(np.float32)).astype(BF))
    return d
def setup_inputs_zeros(rng):
    d = setup_inputs(rng); v = d["xk"].reshape(N, 128, -1, 4).copy()
    v[np.broadcast_to((rng.random((N, 1, v.shape[2], 1)) < 0.33), v.shape)] = 0
    d["xk"] = v.reshape(d["xk"].shape)
    return d
def reference(cs, sn, xk, wk, xq):
    K = [mx_ref.quantize(tile(rot(layer(wk[j], [mx_ref.quantize(xk[j])]), cs[j].astype(np.float32), sn[j].astype(np.float32)))) for j in range(N)]
    y = np.zeros((N, 128, N * NC), np.float32)
    for r in range(N):
        q = mx_ref.quantize(xq[r])
        for j in range(N):
            y[r][:, NC * j:NC * j + NC] = mx_ref.matmul(K[j], q)
    return {"y": y}

@@ -1,0 +1,232 @@
+from concourse.bass import DstId, RemoteDMATransfer
+from concourse.mybir import dt, AluOpType, ActivationFunctionType
+
+WORLD = 256
+N, NC, KC = 4, 384, 128
+HALF = NC // 2
+SCALE = 0.019
+
+SCRATCH = {
+    "xkb": ("sbuf", [128, 512], "bfloat16"),
+    "wkb": ("sbuf", [128, 2048], "bfloat16"),
+    "xqb": ("sbuf", [128, 4 * NC], "bfloat16"),
+    "csb": ("sbuf", [128, KC], "bfloat16"),
+    "snb": ("sbuf", [128, KC], "bfloat16"),
+    "xkc": ("sbuf", [128, KC], "float8_e4m3fn_x4"),
+    "xks": ("sbuf", [128, KC], "uint8"),
+    "wkc": ("sbuf", [128, 4 * KC], "float8_e4m3fn_x4"),
+    "wks": ("sbuf", [128, 4 * KC], "uint8"),
+    "xqc": ("sbuf", [128, NC], "float8_e4m3fn_x4"),
+    "xqs": ("sbuf", [128, NC], "uint8"),
+    "kt": ("sbuf", [128, 512], "bfloat16"),
+    "yb": ("sbuf", [128, N * NC], "float32"),
+    "z": ("psum", [128, 2048], "float32"),
+    "yp": ("psum", [128, 2048], "float32"),
+}
+for _p in range(2):
+    SCRATCH["zz%d" % _p] = ("sbuf", [128, 2 * KC], "float32")
+    for _h in range(2):
+        SCRATCH["ad%d%d" % (_p, _h)] = ("sbuf", [128, 2 * KC], "float32")
+        SCRATCH["ro%d%d" % (_p, _h)] = ("sbuf", [128, 2 * KC], "float32")
+for _j in range(N):
+    SCRATCH["kc%d" % _j] = ("sbuf", [128, KC], "float8_e4m3fn_x4")
+    SCRATCH["ks%d" % _j] = ("sbuf", [128, KC], "uint8")
+
+SEMAPHORES = (["l_xk", "l_cs", "l_sn", "l_xq", "q_xk", "q_k", "q_xq", "relay_in", "sent_far", "sent_peer", "st_last"]
+              + ["l_wk%d" % i for i in range(4)] + ["q_wk%d" % i for i in range(4)] + ["mm%d" % i for i in range(4)]
+              + ["zero%d" % p for p in range(2)] + ["cz%d" % p for p in range(2)] + ["rt%d" % b for b in range(4)]
+              + ["ev%d" % b for b in range(4)] + ["pr%d" % b for b in range(4)] + ["sc%d" % b for b in range(4)]
+              + ["arr%d" % j for j in range(N)]
+              + ["%s%d" % (s, k) for s in ("bl", "br", "cl", "cr", "st") for k in range(N)])
+
+
+def engines(mask):
+    return [1 << e for e in range(16) if mask >> e & 1]
+
+
+def count(mask):
+    return len(engines(mask))
+
+
+def routes(src, T, topo):
+    others = [d for d in T.cores if d != src]
+    peers = [d for d in others if topo.may_write(src, d)]
+    far = [d for d in others if not topo.may_write(src, d)]
+    ports = [q for q in range(WORLD) if q != src and topo.host(q) == topo.host(src) and topo.chip(q) == topo.chip(src)
+             and all(topo.may_write(q, d) for d in far)]
+    near_die = [q for q in ports if topo.die(q) == topo.die(src)]
+    far_die = [q for q in ports if topo.die(q) != topo.die(src)]
+    via = {}
+    for d in far:
+        via[d] = near_die[:2] if topo.host(d) == topo.host(src) else far_die[:2]
+    return peers, via
+
+
+def codes(T, j):
+    return T["kc%d" % j][:, 0:KC].bitcast(dt.uint8)
+
+
+def plane(T, j):
+    return T["ks%d" % j][:, 0:KC]
+
+
+def forward(g, core, T, topo):
+    for src in T.cores:
+        if topo.host(src) != topo.host(core) or topo.chip(src) != topo.chip(core):
+            continue
+        j = T.rank_of(src)
+        via = routes(src, T, topo)[1]
+        for dst in via:
+            for piece, port in zip((codes, plane), via[dst]):
+                if port != core:
+                    continue
+                rid, pid = topo.addr(dst, core)
+                m = topo.mask(core, dst)
+                g.wait_ge(T.sem.relay_in, count(topo.mask(src, core)) // 2)
+                g.remote_dma(out_ap=piece(T, j), in_ap=piece(T, j), remote_sem=T.sem["arr%d" % j],
+                             local_sem=T.sem.sent_far, pid=pid, routing_id=rid, dma_engine_mask=m)
+                g.wait_ge(T.sem.sent_far, count(m))
+
+
+def rank_program(g, core, T, topo):
+    r = T.rank_of(core)
+    if r is None:
+        forward(g, core, T, topo)
+        return
+    S = T.sem
+    v, t, a, s = g.vector, g.tensor, g.scalar, g.sync
+    copy = ActivationFunctionType.Copy
+    mult, add, sub = AluOpType.mult, AluOpType.add, AluOpType.subtract
+    peers, via = routes(core, T, topo)
+    peer = peers[0]
+    far = sorted(via, key=lambda d: topo.host(d) != topo.host(core))
+    order = [r, T.rank_of(peer)] + [T.rank_of(d) for d in far]
+    odd, even = slice(1, 2 * KC, 2), slice(0, 2 * KC, 2)
+
+    def wk(i):
+        return slice(512 * i, 512 * i + 512)
+
+    def wt(i):
+        return slice(KC * i, KC * i + KC)
+
+    def Z(i):
+        return T.z[:, 512 * i:512 * i + KC]
+
+    s.dma_start(T.xkb[:, :], T.xk[:, :]).then_inc(S.l_xk, 16)
+    a.dma_start(T.wkb[:, wk(0)], T.wk[:, wk(0)]).then_inc(S.l_wk0, 16)
+    s.dma_start(T.wkb[:, wk(1)], T.wk[:, wk(1)]).then_inc(S.l_wk1, 16)
+    a.dma_start(T.snb[:, :], T.sn[:, :]).then_inc(S.l_sn, 16)
+    s.dma_start(T.csb[:, :], T.cs[:, :]).then_inc(S.l_cs, 16)
+    a.dma_start(T.wkb[:, wk(2)], T.wk[:, wk(2)]).then_inc(S.l_wk2, 16)
+    s.dma_start(T.wkb[:, wk(3)], T.wk[:, wk(3)]).then_inc(S.l_wk3, 16)
+    s.wait_ge(S.l_wk1, 16)
+    s.dma_start(T.xqb[:, :], T.xq[:, :]).then_inc(S.l_xq, 16)
+
+    t.wait_ge(S.q_xk, 1)
+    for i in range(4):
+        t.wait_ge(S["q_wk%d" % i], 1)
+        t.matmul_mx(Z(i), T.wkc[:, wt(i)], T.wks[:, wt(i)], T.xkc[:, 0:KC], T.xks[:, 0:KC], True, True
+                    ).then_inc(S["mm%d" % i], 1)
+
+    a.wait_ge(S.l_sn, 16)
+    for p in range(2):
+        a.activation(T["ad%d1" % p][:, even], T.snb[:, :], copy).then_inc(S["ev%d" % (2 * p + 1)], 1)
+    a.wait_ge(S.l_cs, 16)
+    for p in range(2):
+        a.activation(T["ad%d0" % p][:, even], T.csb[:, :], copy, scale=-1.0).then_inc(S["ev%d" % (2 * p)], 1)
+    for p in range(2):
+        a.wait_ge(S["zero%d" % p], 1)
+        a.wait_ge(S["mm%d" % (2 * p)], 1)
+        a.activation(T["zz%d" % p][:, odd], Z(2 * p), copy).then_inc(S["cz%d" % p], 1)
+    for b in range(4):
+        a.wait_ge(S["sc%d" % b], 1)
+        a.activation(T.kt[:, b:512:4], T["ro%d%d" % (b // 2, b % 2)][:, odd], copy, scale=SCALE).then_inc(S["rt%d" % b], 1)
+
+    def quant_wk(i):
+        v.wait_ge(S["l_wk%d" % i], 16)
+        v.quantize_mx(T.wkc[:, wt(i)], T.wks[:, wt(i)], T.wkb[:, wk(i)]).then_inc(S["q_wk%d" % i], 1)
+
+    def products(p):
+        v.wait_ge(S["mm%d" % (2 * p + 1)], 1)
+        for h, (load, ang) in enumerate((("l_sn", T.snb), ("l_cs", T.csb))):
+            v.wait_ge(S[load], 16)
+            v.tensor_tensor(T["ad%d%d" % (p, h)][:, odd], Z(2 * p + 1), ang[:, :], mult).then_inc(S["pr%d" % (2 * p + h)], 1)
+
+    def scan(b):
+        p, h = b // 2, b % 2
+        v.wait_ge(S["pr%d" % b], 1)
+        v.wait_ge(S["ev%d" % b], 1)
+        v.wait_ge(S["cz%d" % p], 1)
+        v.tensor_tensor_scan(T["ro%d%d" % (p, h)][:, :], T["zz%d" % p][:, :], T["ad%d%d" % (p, h)][:, :], 0.0,
+                             mult, add if h else sub).then_inc(S["sc%d" % b], 1)
+
+    for p in range(2):
+        v.memset(T["zz%d" % p][:, :], 0.0).then_inc(S["zero%d" % p], 1)
+    v.wait_ge(S.l_xk, 16)
+    v.quantize_mx(T.xkc[:, :], T.xks[:, :], T.xkb[:, :]).then_inc(S.q_xk, 1)
+    quant_wk(0)
+    quant_wk(1)
+    quant_wk(2)
+    products(0)
+    scan(0)
+    quant_wk(3)
+    scan(1)
+    products(1)
+    scan(2)
+    scan(3)
+    for b in range(4):
+        v.wait_ge(S["rt%d" % b], 1)
+    v.quantize_mx(T["kc%d" % r][:, :], T["ks%d" % r][:, :], T.kt[:, :]).then_inc(S.q_k, 1)
+    v.wait_ge(S.l_xq, 16)
+    v.quantize_mx(T.xqc[:, :], T.xqs[:, :], T.xqb[:, :]).then_inc(S.q_xq, 1)
+
+    g.wait_ge(S.q_k, 1)
+    far_engines = 0
+    for which, piece in enumerate((codes, plane)):
+        moves = []
+        for k, d in enumerate(far):
+            port = via[d][which]
+            m = sum(engines(topo.mask(core, port))[1 - k::2])
+            rid, pid = topo.addr(port, core)
+            moves.append(RemoteDMATransfer(dst_ids=[DstId(rid=rid, pnc=pid)], dma_engine_mask=m, remote_sem=S.relay_in,
+                                           src=piece(T, r), dst=piece(T, r)))
+            far_engines += count(m)
+        g.remote_dma_fused(moves, local_sem=S.sent_far)
+    rid, pid = topo.addr(peer, core)
+    m = topo.mask(core, peer)
+    for piece in (codes, plane):
+        g.remote_dma(out_ap=piece(T, r), in_ap=piece(T, r), remote_sem=S["arr%d" % r], local_sem=S.sent_peer,
+                     pid=pid, routing_id=rid, dma_engine_mask=m)
+    g.wait_ge(S.sent_far, far_engines)
+    g.wait_ge(S.sent_peer, 2 * count(m))
+
+    t.wait_ge(S.q_k, 1)
+    t.wait_ge(S.q_xq, 1)
+    s.wait_ge(S.sent_far, far_engines)
+    for n, j in enumerate(order):
+        banks, at = (T.yp, 1024 * n) if n < 2 else (T.z, 1024 * (n - 2))
+        left, right = slice(NC * j, NC * j + HALF), slice(NC * j + HALF, NC * j + NC)
+        if n == 1:
+            t.wait_ge(S["arr%d" % j], 2 * count(topo.mask(peer, core)))
+        if n > 1:
+            ports = routes(T.cores[j], T, topo)[1][core]
+            t.wait_ge(S["arr%d" % j], sum(count(topo.mask(q, core)) for q in ports))
+        for h, sem in enumerate(("bl", "br")):
+            t.matmul_mx(banks[:, at + 512 * h:at + 512 * h + HALF], T["kc%d" % j][:, 0:KC], T["ks%d" % j][:, 0:KC],
+                        T.xqc[:, HALF * h:HALF * h + HALF], T.xqs[:, HALF * h:HALF * h + HALF], True, True
+                        ).then_inc(S["%s%d" % (sem, n)], 1)
+        v.wait_ge(S["bl%d" % n], 1)
+        v.tensor_copy(T.yb[:, left], banks[:, at:at + HALF]).then_inc(S["cl%d" % n], 1)
+        a.wait_ge(S["br%d" % n], 1)
+        a.activation(T.yb[:, right], banks[:, at + 512:at + 512 + HALF], copy).then_inc(S["cr%d" % n], 1)
+        s.wait_ge(S["cl%d" % n], 1)
+        if n < N - 1:
+            s.wait_ge(S["cr%d" % n], 1)
+            s.dma_start(T.y[:, NC * j:NC * j + NC], T.yb[:, NC * j:NC * j + NC]).then_inc(S["st%d" % n], 16)
+        else:
+            s.dma_start(T.y[:, left], T.yb[:, left]).then_inc(S["st%d" % n], 16)
+            a.wait_ge(S["cr%d" % n], 1)
+            a.dma_start(T.y[:, right], T.yb[:, right]).then_inc(S.st_last, 16)
+    for n in range(N):
+        s.wait_ge(S["st%d" % n], 16)
+    a.wait_ge(S.st_last, 16)

@@ -3,7 +3,10 @@ from concourse.mybir import dt, AluOpType, ActivationFunctionType
 
 WORLD = 256
 N, NC, KC = 4, 384, 128
-HALF = NC // 2
+CUT = 192
+AHEAD = 48
+MID = (AHEAD + KC) // 2
+PARTS = ((0, AHEAD), (AHEAD, KC))
 SCALE = 0.019
 
 SCRATCH = {
@@ -19,6 +22,8 @@ SCRATCH = {
     "xqc": ("sbuf", [128, NC], "float8_e4m3fn_x4"),
     "xqs": ("sbuf", [128, NC], "uint8"),
     "kt": ("sbuf", [128, 512], "bfloat16"),
+    "kca": ("sbuf", [128, KC], "float8_e4m3fn_x4"),
+    "ksa": ("sbuf", [128, KC], "uint8"),
     "yb": ("sbuf", [128, N * NC], "float32"),
     "z": ("psum", [128, 2048], "float32"),
     "yp": ("psum", [128, 2048], "float32"),
@@ -32,10 +37,12 @@ for _j in range(N):
     SCRATCH["kc%d" % _j] = ("sbuf", [128, KC], "float8_e4m3fn_x4")
     SCRATCH["ks%d" % _j] = ("sbuf", [128, KC], "uint8")
 
-SEMAPHORES = (["l_xk", "l_cs", "l_sn", "l_xq", "q_xk", "q_k", "q_xq", "relay_in", "sent_far", "sent_peer", "st_last"]
+SEMAPHORES = (["l_xk", "l_cs", "l_sn", "l_xq", "q_xk", "q_k", "q_xq", "ahead_in", "rest_in", "sent_far", "sent_peer", "st_last",
+               "k_zero", "q_ahead", "sc_end", "rt_end"]
               + ["l_wk%d" % i for i in range(4)] + ["q_wk%d" % i for i in range(4)] + ["mm%d" % i for i in range(4)]
-              + ["zero%d" % p for p in range(2)] + ["cz%d" % p for p in range(2)] + ["rt%d" % b for b in range(4)]
-              + ["ev%d" % b for b in range(4)] + ["pr%d" % b for b in range(4)] + ["sc%d" % b for b in range(4)]
+              + ["zero%d" % p for p in range(2)] + ["ev%d" % b for b in range(4)]
+              + ["cz%d%d" % (p, x) for p in range(2) for x in range(2)]
+              + ["%s%d%d" % (s, b, x) for s in ("pr", "sc", "rt") for b in range(4) for x in range(2)]
               + ["arr%d" % j for j in range(N)]
               + ["%s%d" % (s, k) for s in ("bl", "br", "cl", "cr", "st") for k in range(N)])
 
@@ -62,12 +69,16 @@ def routes(src, T, topo):
     return peers, via
 
 
-def codes(T, j):
-    return T["kc%d" % j][:, 0:KC].bitcast(dt.uint8)
+def codes(buf, lo, hi):
+    return buf[:, lo:hi].bitcast(dt.uint8)
 
 
-def plane(T, j):
-    return T["ks%d" % j][:, 0:KC]
+def first(kc, ks, k):
+    return ks[:, 0:AHEAD] if k else codes(kc, 0, AHEAD)
+
+
+def rest(kc, ks, k):
+    return ks[:, AHEAD:KC] if k else codes(kc, AHEAD, KC)
 
 
 def forward(g, core, T, topo):
@@ -77,15 +88,17 @@ def forward(g, core, T, topo):
         j = T.rank_of(src)
         via = routes(src, T, topo)[1]
         for dst in via:
-            for piece, port in zip((codes, plane), via[dst]):
+            for k, port in enumerate(via[dst]):
                 if port != core:
                     continue
                 rid, pid = topo.addr(dst, core)
                 m = topo.mask(core, dst)
-                g.wait_ge(T.sem.relay_in, count(topo.mask(src, core)) // 2)
-                g.remote_dma(out_ap=piece(T, j), in_ap=piece(T, j), remote_sem=T.sem["arr%d" % j],
-                             local_sem=T.sem.sent_far, pid=pid, routing_id=rid, dma_engine_mask=m)
-                g.wait_ge(T.sem.sent_far, count(m))
+                for piece, sem in ((first, T.sem.ahead_in), (rest, T.sem.rest_in)):
+                    part = piece(T["kc%d" % j], T["ks%d" % j], k)
+                    g.wait_ge(sem, count(topo.mask(src, core)) // 2)
+                    g.remote_dma(out_ap=part, in_ap=part, remote_sem=T.sem["arr%d" % j], local_sem=T.sem.sent_far,
+                                 pid=pid, routing_id=rid, dma_engine_mask=m)
+                g.wait_ge(T.sem.sent_far, 2 * count(m))
 
 
 def rank_program(g, core, T, topo):
@@ -101,7 +114,8 @@ def rank_program(g, core, T, topo):
     peer = peers[0]
     far = sorted(via, key=lambda d: topo.host(d) != topo.host(core))
     order = [r, T.rank_of(peer)] + [T.rank_of(d) for d in far]
-    odd, even = slice(1, 2 * KC, 2), slice(0, 2 * KC, 2)
+    even = slice(0, 2 * KC, 2)
+    kc, ks = T["kc%d" % r], T["ks%d" % r]
 
     def wk(i):
         return slice(512 * i, 512 * i + 512)
@@ -109,24 +123,35 @@ def rank_program(g, core, T, topo):
     def wt(i):
         return slice(KC * i, KC * i + KC)
 
-    def Z(i):
-        return T.z[:, 512 * i:512 * i + KC]
+    def odd(lo, hi):
+        return slice(2 * lo + 1, 2 * hi, 2)
+
+    def Z(i, lo, hi):
+        return T.z[:, 512 * i + lo:512 * i + hi]
 
     s.dma_start(T.xkb[:, :], T.xk[:, :]).then_inc(S.l_xk, 16)
-    a.dma_start(T.wkb[:, wk(0)], T.wk[:, wk(0)]).then_inc(S.l_wk0, 16)
-    s.dma_start(T.wkb[:, wk(1)], T.wk[:, wk(1)]).then_inc(S.l_wk1, 16)
+    a.dma_start(T.wkb[:, wk(1)], T.wk[:, wk(1)]).then_inc(S.l_wk1, 16)
+    s.dma_start(T.wkb[:, wk(0)], T.wk[:, wk(0)]).then_inc(S.l_wk0, 16)
     a.dma_start(T.snb[:, :], T.sn[:, :]).then_inc(S.l_sn, 16)
-    s.dma_start(T.csb[:, :], T.cs[:, :]).then_inc(S.l_cs, 16)
-    a.dma_start(T.wkb[:, wk(2)], T.wk[:, wk(2)]).then_inc(S.l_wk2, 16)
+    a.dma_start(T.csb[:, :], T.cs[:, :]).then_inc(S.l_cs, 16)
     s.dma_start(T.wkb[:, wk(3)], T.wk[:, wk(3)]).then_inc(S.l_wk3, 16)
+    s.dma_start(T.wkb[:, wk(2)], T.wk[:, wk(2)]).then_inc(S.l_wk2, 16)
     s.wait_ge(S.l_wk1, 16)
     s.dma_start(T.xqb[:, :], T.xq[:, :]).then_inc(S.l_xq, 16)
 
     t.wait_ge(S.q_xk, 1)
-    for i in range(4):
+    for i in (1, 0, 3, 2):
         t.wait_ge(S["q_wk%d" % i], 1)
-        t.matmul_mx(Z(i), T.wkc[:, wt(i)], T.wks[:, wt(i)], T.xkc[:, 0:KC], T.xks[:, 0:KC], True, True
+        t.matmul_mx(Z(i, 0, KC), T.wkc[:, wt(i)], T.wks[:, wt(i)], T.xkc[:, 0:KC], T.xks[:, 0:KC], True, True
                     ).then_inc(S["mm%d" % i], 1)
+
+    def scaled(b, lo, hi, eng, src, dst):
+        eng.wait_ge(S[src], 1)
+        of, to = T["ro%d%d" % (b // 2, b % 2)][:, odd(lo, hi)], T.kt[:, 4 * lo + b:4 * hi:4]
+        if eng is a:
+            a.activation(to, of, copy, scale=SCALE).then_inc(S[dst], 1)
+        else:
+            v.tensor_scalar(to, of, SCALE, None, mult).then_inc(S[dst], 1)
 
     a.wait_ge(S.l_sn, 16)
     for p in range(2):
@@ -134,68 +159,90 @@ def rank_program(g, core, T, topo):
     a.wait_ge(S.l_cs, 16)
     for p in range(2):
         a.activation(T["ad%d0" % p][:, even], T.csb[:, :], copy, scale=-1.0).then_inc(S["ev%d" % (2 * p)], 1)
-    for p in range(2):
-        a.wait_ge(S["zero%d" % p], 1)
-        a.wait_ge(S["mm%d" % (2 * p)], 1)
-        a.activation(T["zz%d" % p][:, odd], Z(2 * p), copy).then_inc(S["cz%d" % p], 1)
+    for x, (lo, hi) in enumerate(PARTS):
+        for p in range(2):
+            a.wait_ge(S["zero%d" % p], 1)
+            a.wait_ge(S["mm%d" % (2 * p)], 1)
+            a.activation(T["zz%d" % p][:, odd(lo, hi)], Z(2 * p, lo, hi), copy).then_inc(S["cz%d%d" % (p, x)], 1)
+    a.wait_ge(S.k_zero, 1)
     for b in range(4):
-        a.wait_ge(S["sc%d" % b], 1)
-        a.activation(T.kt[:, b:512:4], T["ro%d%d" % (b // 2, b % 2)][:, odd], copy, scale=SCALE).then_inc(S["rt%d" % b], 1)
+        scaled(b, 0, AHEAD, a, "sc%d0" % b, "rt%d0" % b)
+    a.wait_ge(S.q_ahead, 1)
+    for b in range(4):
+        scaled(b, AHEAD, KC if b < 3 else MID, a, "sc%d1" % b, "rt%d1" % b)
 
     def quant_wk(i):
         v.wait_ge(S["l_wk%d" % i], 16)
         v.quantize_mx(T.wkc[:, wt(i)], T.wks[:, wt(i)], T.wkb[:, wk(i)]).then_inc(S["q_wk%d" % i], 1)
 
-    def products(p):
-        v.wait_ge(S["mm%d" % (2 * p + 1)], 1)
-        for h, (load, ang) in enumerate((("l_sn", T.snb), ("l_cs", T.csb))):
-            v.wait_ge(S[load], 16)
-            v.tensor_tensor(T["ad%d%d" % (p, h)][:, odd], Z(2 * p + 1), ang[:, :], mult).then_inc(S["pr%d" % (2 * p + h)], 1)
-
-    def scan(b):
+    def product(b, x):
         p, h = b // 2, b % 2
-        v.wait_ge(S["pr%d" % b], 1)
+        lo, hi = PARTS[x]
+        v.wait_ge(S["mm%d" % (2 * p + 1)], 1)
+        v.wait_ge(S.l_cs if h else S.l_sn, 16)
+        v.tensor_tensor(T["ad%d%d" % (p, h)][:, odd(lo, hi)], Z(2 * p + 1, lo, hi), (T.csb if h else T.snb)[:, lo:hi], mult
+                        ).then_inc(S["pr%d%d" % (b, x)], 1)
+
+    def scan(b, x, cuts):
+        p, h = b // 2, b % 2
+        v.wait_ge(S["pr%d%d" % (b, x)], 1)
         v.wait_ge(S["ev%d" % b], 1)
-        v.wait_ge(S["cz%d" % p], 1)
-        v.tensor_tensor_scan(T["ro%d%d" % (p, h)][:, :], T["zz%d" % p][:, :], T["ad%d%d" % (p, h)][:, :], 0.0,
-                             mult, add if h else sub).then_inc(S["sc%d" % b], 1)
+        v.wait_ge(S["cz%d%d" % (p, x)], 1)
+        for sem, lo, hi in cuts:
+            c = slice(2 * lo, 2 * hi)
+            v.tensor_tensor_scan(T["ro%d%d" % (p, h)][:, c], T["zz%d" % p][:, c], T["ad%d%d" % (p, h)][:, c], 0.0,
+                                 mult, add if h else sub).then_inc(S[sem], 1)
 
     for p in range(2):
         v.memset(T["zz%d" % p][:, :], 0.0).then_inc(S["zero%d" % p], 1)
+    v.memset(T.kt[:, :], 0.0).then_inc(S.k_zero, 1)
     v.wait_ge(S.l_xk, 16)
     v.quantize_mx(T.xkc[:, :], T.xks[:, :], T.xkb[:, :]).then_inc(S.q_xk, 1)
-    quant_wk(0)
-    quant_wk(1)
-    quant_wk(2)
-    products(0)
-    scan(0)
-    quant_wk(3)
-    scan(1)
-    products(1)
-    scan(2)
-    scan(3)
+    for i in (1, 0, 3, 2):
+        quant_wk(i)
     for b in range(4):
-        v.wait_ge(S["rt%d" % b], 1)
-    v.quantize_mx(T["kc%d" % r][:, :], T["ks%d" % r][:, :], T.kt[:, :]).then_inc(S.q_k, 1)
+        product(b, 0)
+    for b in range(4):
+        v.wait_ge(S["zero%d" % (b // 2)], 1)
+        scan(b, 0, [("sc%d0" % b, 0, AHEAD)])
+    product(0, 1)
+    v.wait_ge(S.k_zero, 1)
+    for b in range(4):
+        v.wait_ge(S["rt%d0" % b], 1)
+    v.quantize_mx(T.kca[:, :], T.ksa[:, :], T.kt[:, :]).then_inc(S.q_ahead, 1)
+    product(1, 1)
+    scan(0, 1, [("sc01", AHEAD, KC)])
+    scan(1, 1, [("sc11", AHEAD, KC)])
+    product(2, 1)
+    product(3, 1)
+    scan(2, 1, [("sc21", AHEAD, KC)])
+    scan(3, 1, [("sc31", AHEAD, MID), ("sc_end", MID, KC)])
+    v.wait_ge(S.q_ahead, 1)
+    scaled(3, MID, KC, v, "sc_end", "rt_end")
+    v.wait_ge(S.rt_end, 1)
+    for b in range(4):
+        v.wait_ge(S["rt%d1" % b], 1)
+    v.quantize_mx(kc[:, :], ks[:, :], T.kt[:, :]).then_inc(S.q_k, 1)
     v.wait_ge(S.l_xq, 16)
     v.quantize_mx(T.xqc[:, :], T.xqs[:, :], T.xqb[:, :]).then_inc(S.q_xq, 1)
 
-    g.wait_ge(S.q_k, 1)
     far_engines = 0
-    for which, piece in enumerate((codes, plane)):
-        moves = []
-        for k, d in enumerate(far):
-            port = via[d][which]
-            m = sum(engines(topo.mask(core, port))[1 - k::2])
-            rid, pid = topo.addr(port, core)
-            moves.append(RemoteDMATransfer(dst_ids=[DstId(rid=rid, pnc=pid)], dma_engine_mask=m, remote_sem=S.relay_in,
-                                           src=piece(T, r), dst=piece(T, r)))
-            far_engines += count(m)
-        g.remote_dma_fused(moves, local_sem=S.sent_far)
+    for ready, piece, src, sem in ((S.q_ahead, first, (T.kca, T.ksa), S.ahead_in), (S.q_k, rest, (kc, ks), S.rest_in)):
+        g.wait_ge(ready, 1)
+        for k in range(2):
+            moves = []
+            for f, d in enumerate(far):
+                port = via[d][k]
+                rid, pid = topo.addr(port, core)
+                m = sum(engines(topo.mask(core, port))[1 - f::2])
+                moves.append(RemoteDMATransfer(dst_ids=[DstId(rid=rid, pnc=pid)], dma_engine_mask=m, remote_sem=sem,
+                                               src=piece(src[0], src[1], k), dst=piece(kc, ks, k)))
+                far_engines += count(m)
+            g.remote_dma_fused(moves, local_sem=S.sent_far)
     rid, pid = topo.addr(peer, core)
     m = topo.mask(core, peer)
-    for piece in (codes, plane):
-        g.remote_dma(out_ap=piece(T, r), in_ap=piece(T, r), remote_sem=S["arr%d" % r], local_sem=S.sent_peer,
+    for piece in (codes(kc, 0, KC), ks[:, 0:KC]):
+        g.remote_dma(out_ap=piece, in_ap=piece, remote_sem=S["arr%d" % r], local_sem=S.sent_peer,
                      pid=pid, routing_id=rid, dma_engine_mask=m)
     g.wait_ge(S.sent_far, far_engines)
     g.wait_ge(S.sent_peer, 2 * count(m))
@@ -205,20 +252,19 @@ def rank_program(g, core, T, topo):
     s.wait_ge(S.sent_far, far_engines)
     for n, j in enumerate(order):
         banks, at = (T.yp, 1024 * n) if n < 2 else (T.z, 1024 * (n - 2))
-        left, right = slice(NC * j, NC * j + HALF), slice(NC * j + HALF, NC * j + NC)
+        left, right = slice(NC * j, NC * j + CUT), slice(NC * j + CUT, NC * j + NC)
         if n == 1:
             t.wait_ge(S["arr%d" % j], 2 * count(topo.mask(peer, core)))
         if n > 1:
             ports = routes(T.cores[j], T, topo)[1][core]
-            t.wait_ge(S["arr%d" % j], sum(count(topo.mask(q, core)) for q in ports))
-        for h, sem in enumerate(("bl", "br")):
-            t.matmul_mx(banks[:, at + 512 * h:at + 512 * h + HALF], T["kc%d" % j][:, 0:KC], T["ks%d" % j][:, 0:KC],
-                        T.xqc[:, HALF * h:HALF * h + HALF], T.xqs[:, HALF * h:HALF * h + HALF], True, True
-                        ).then_inc(S["%s%d" % (sem, n)], 1)
+            t.wait_ge(S["arr%d" % j], 2 * sum(count(topo.mask(q, core)) for q in ports))
+        for sem, bank, lo, hi in (("bl", at, 0, CUT), ("br", at + 512, CUT, NC)):
+            t.matmul_mx(banks[:, bank:bank + hi - lo], T["kc%d" % j][:, 0:KC], T["ks%d" % j][:, 0:KC],
+                        T.xqc[:, lo:hi], T.xqs[:, lo:hi], True, True).then_inc(S["%s%d" % (sem, n)], 1)
         v.wait_ge(S["bl%d" % n], 1)
-        v.tensor_copy(T.yb[:, left], banks[:, at:at + HALF]).then_inc(S["cl%d" % n], 1)
+        v.tensor_copy(T.yb[:, left], banks[:, at:at + CUT]).then_inc(S["cl%d" % n], 1)
         a.wait_ge(S["br%d" % n], 1)
-        a.activation(T.yb[:, right], banks[:, at + 512:at + 512 + HALF], copy).then_inc(S["cr%d" % n], 1)
+        a.activation(T.yb[:, right], banks[:, at + 512:at + 512 + NC - CUT], copy).then_inc(S["cr%d" % n], 1)
         s.wait_ge(S["cl%d" % n], 1)
         if n < N - 1:
             s.wait_ge(S["cr%d" % n], 1)

from concourse.bass import DstId, RemoteDMATransfer
from concourse.mybir import dt, AluOpType, ActivationFunctionType

WORLD = 256
N, NC, KC = 4, 384, 128
CUT = 192
AHEAD = 48
MID = (AHEAD + KC) // 2
PARTS = ((0, AHEAD), (AHEAD, KC))
SCALE = 0.019

SCRATCH = {
    "xkb": ("sbuf", [128, 512], "bfloat16"),
    "wkb": ("sbuf", [128, 2048], "bfloat16"),
    "xqb": ("sbuf", [128, 4 * NC], "bfloat16"),
    "csb": ("sbuf", [128, KC], "bfloat16"),
    "snb": ("sbuf", [128, KC], "bfloat16"),
    "xkc": ("sbuf", [128, KC], "float8_e4m3fn_x4"),
    "xks": ("sbuf", [128, KC], "uint8"),
    "wkc": ("sbuf", [128, 4 * KC], "float8_e4m3fn_x4"),
    "wks": ("sbuf", [128, 4 * KC], "uint8"),
    "xqc": ("sbuf", [128, NC], "float8_e4m3fn_x4"),
    "xqs": ("sbuf", [128, NC], "uint8"),
    "kt": ("sbuf", [128, 512], "bfloat16"),
    "kca": ("sbuf", [128, KC], "float8_e4m3fn_x4"),
    "ksa": ("sbuf", [128, KC], "uint8"),
    "yb": ("sbuf", [128, N * NC], "float32"),
    "z": ("psum", [128, 2048], "float32"),
    "yp": ("psum", [128, 2048], "float32"),
}
for _p in range(2):
    SCRATCH["zz%d" % _p] = ("sbuf", [128, 2 * KC], "float32")
    for _h in range(2):
        SCRATCH["ad%d%d" % (_p, _h)] = ("sbuf", [128, 2 * KC], "float32")
        SCRATCH["ro%d%d" % (_p, _h)] = ("sbuf", [128, 2 * KC], "float32")
for _j in range(N):
    SCRATCH["kc%d" % _j] = ("sbuf", [128, KC], "float8_e4m3fn_x4")
    SCRATCH["ks%d" % _j] = ("sbuf", [128, KC], "uint8")

SEMAPHORES = (["l_xk", "l_cs", "l_sn", "l_xq", "q_xk", "q_k", "q_xq", "ahead_in", "rest_in", "sent_far", "sent_peer", "st_last",
               "k_zero", "q_ahead", "sc_end", "rt_end"]
              + ["l_wk%d" % i for i in range(4)] + ["q_wk%d" % i for i in range(4)] + ["mm%d" % i for i in range(4)]
              + ["zero%d" % p for p in range(2)] + ["ev%d" % b for b in range(4)]
              + ["cz%d%d" % (p, x) for p in range(2) for x in range(2)]
              + ["%s%d%d" % (s, b, x) for s in ("pr", "sc", "rt") for b in range(4) for x in range(2)]
              + ["arr%d" % j for j in range(N)]
              + ["%s%d" % (s, k) for s in ("bl", "br", "cl", "cr", "st") for k in range(N)])


def engines(mask):
    return [1 << e for e in range(16) if mask >> e & 1]


def count(mask):
    return len(engines(mask))


def routes(src, T, topo):
    others = [d for d in T.cores if d != src]
    peers = [d for d in others if topo.may_write(src, d)]
    far = [d for d in others if not topo.may_write(src, d)]
    ports = [q for q in range(WORLD) if q != src and topo.host(q) == topo.host(src) and topo.chip(q) == topo.chip(src)
             and all(topo.may_write(q, d) for d in far)]
    near_die = [q for q in ports if topo.die(q) == topo.die(src)]
    far_die = [q for q in ports if topo.die(q) != topo.die(src)]
    via = {}
    for d in far:
        via[d] = near_die[:2] if topo.host(d) == topo.host(src) else far_die[:2]
    return peers, via


def codes(buf, lo, hi):
    return buf[:, lo:hi].bitcast(dt.uint8)


def first(kc, ks, k):
    return ks[:, 0:AHEAD] if k else codes(kc, 0, AHEAD)


def rest(kc, ks, k):
    return ks[:, AHEAD:KC] if k else codes(kc, AHEAD, KC)


def forward(g, core, T, topo):
    for src in T.cores:
        if topo.host(src) != topo.host(core) or topo.chip(src) != topo.chip(core):
            continue
        j = T.rank_of(src)
        via = routes(src, T, topo)[1]
        for dst in via:
            for k, port in enumerate(via[dst]):
                if port != core:
                    continue
                rid, pid = topo.addr(dst, core)
                m = topo.mask(core, dst)
                for piece, sem in ((first, T.sem.ahead_in), (rest, T.sem.rest_in)):
                    part = piece(T["kc%d" % j], T["ks%d" % j], k)
                    g.wait_ge(sem, count(topo.mask(src, core)) // 2)
                    g.remote_dma(out_ap=part, in_ap=part, remote_sem=T.sem["arr%d" % j], local_sem=T.sem.sent_far,
                                 pid=pid, routing_id=rid, dma_engine_mask=m)
                g.wait_ge(T.sem.sent_far, 2 * count(m))


def rank_program(g, core, T, topo):
    r = T.rank_of(core)
    if r is None:
        forward(g, core, T, topo)
        return
    S = T.sem
    v, t, a, s = g.vector, g.tensor, g.scalar, g.sync
    copy = ActivationFunctionType.Copy
    mult, add, sub = AluOpType.mult, AluOpType.add, AluOpType.subtract
    peers, via = routes(core, T, topo)
    peer = peers[0]
    far = sorted(via, key=lambda d: topo.host(d) != topo.host(core))
    order = [r, T.rank_of(peer)] + [T.rank_of(d) for d in far]
    even = slice(0, 2 * KC, 2)
    kc, ks = T["kc%d" % r], T["ks%d" % r]

    def wk(i):
        return slice(512 * i, 512 * i + 512)

    def wt(i):
        return slice(KC * i, KC * i + KC)

    def odd(lo, hi):
        return slice(2 * lo + 1, 2 * hi, 2)

    def Z(i, lo, hi):
        return T.z[:, 512 * i + lo:512 * i + hi]

    s.dma_start(T.xkb[:, :], T.xk[:, :]).then_inc(S.l_xk, 16)
    a.dma_start(T.wkb[:, wk(1)], T.wk[:, wk(1)]).then_inc(S.l_wk1, 16)
    s.dma_start(T.wkb[:, wk(0)], T.wk[:, wk(0)]).then_inc(S.l_wk0, 16)
    a.dma_start(T.snb[:, :], T.sn[:, :]).then_inc(S.l_sn, 16)
    a.dma_start(T.csb[:, :], T.cs[:, :]).then_inc(S.l_cs, 16)
    s.dma_start(T.wkb[:, wk(3)], T.wk[:, wk(3)]).then_inc(S.l_wk3, 16)
    s.dma_start(T.wkb[:, wk(2)], T.wk[:, wk(2)]).then_inc(S.l_wk2, 16)
    s.wait_ge(S.l_wk1, 16)
    s.dma_start(T.xqb[:, :], T.xq[:, :]).then_inc(S.l_xq, 16)

    t.wait_ge(S.q_xk, 1)
    for i in (1, 0, 3, 2):
        t.wait_ge(S["q_wk%d" % i], 1)
        t.matmul_mx(Z(i, 0, KC), T.wkc[:, wt(i)], T.wks[:, wt(i)], T.xkc[:, 0:KC], T.xks[:, 0:KC], True, True
                    ).then_inc(S["mm%d" % i], 1)

    def scaled(b, lo, hi, eng, src, dst):
        eng.wait_ge(S[src], 1)
        of, to = T["ro%d%d" % (b // 2, b % 2)][:, odd(lo, hi)], T.kt[:, 4 * lo + b:4 * hi:4]
        if eng is a:
            a.activation(to, of, copy, scale=SCALE).then_inc(S[dst], 1)
        else:
            v.tensor_scalar(to, of, SCALE, None, mult).then_inc(S[dst], 1)

    a.wait_ge(S.l_sn, 16)
    for p in range(2):
        a.activation(T["ad%d1" % p][:, even], T.snb[:, :], copy).then_inc(S["ev%d" % (2 * p + 1)], 1)
    a.wait_ge(S.l_cs, 16)
    for p in range(2):
        a.activation(T["ad%d0" % p][:, even], T.csb[:, :], copy, scale=-1.0).then_inc(S["ev%d" % (2 * p)], 1)
    for x, (lo, hi) in enumerate(PARTS):
        for p in range(2):
            a.wait_ge(S["zero%d" % p], 1)
            a.wait_ge(S["mm%d" % (2 * p)], 1)
            a.activation(T["zz%d" % p][:, odd(lo, hi)], Z(2 * p, lo, hi), copy).then_inc(S["cz%d%d" % (p, x)], 1)
    a.wait_ge(S.k_zero, 1)
    for b in range(4):
        scaled(b, 0, AHEAD, a, "sc%d0" % b, "rt%d0" % b)
    a.wait_ge(S.q_ahead, 1)
    for b in range(4):
        scaled(b, AHEAD, KC if b < 3 else MID, a, "sc%d1" % b, "rt%d1" % b)

    def quant_wk(i):
        v.wait_ge(S["l_wk%d" % i], 16)
        v.quantize_mx(T.wkc[:, wt(i)], T.wks[:, wt(i)], T.wkb[:, wk(i)]).then_inc(S["q_wk%d" % i], 1)

    def product(b, x):
        p, h = b // 2, b % 2
        lo, hi = PARTS[x]
        v.wait_ge(S["mm%d" % (2 * p + 1)], 1)
        v.wait_ge(S.l_cs if h else S.l_sn, 16)
        v.tensor_tensor(T["ad%d%d" % (p, h)][:, odd(lo, hi)], Z(2 * p + 1, lo, hi), (T.csb if h else T.snb)[:, lo:hi], mult
                        ).then_inc(S["pr%d%d" % (b, x)], 1)

    def scan(b, x, cuts):
        p, h = b // 2, b % 2
        v.wait_ge(S["pr%d%d" % (b, x)], 1)
        v.wait_ge(S["ev%d" % b], 1)
        v.wait_ge(S["cz%d%d" % (p, x)], 1)
        for sem, lo, hi in cuts:
            c = slice(2 * lo, 2 * hi)
            v.tensor_tensor_scan(T["ro%d%d" % (p, h)][:, c], T["zz%d" % p][:, c], T["ad%d%d" % (p, h)][:, c], 0.0,
                                 mult, add if h else sub).then_inc(S[sem], 1)

    for p in range(2):
        v.memset(T["zz%d" % p][:, :], 0.0).then_inc(S["zero%d" % p], 1)
    v.memset(T.kt[:, :], 0.0).then_inc(S.k_zero, 1)
    v.wait_ge(S.l_xk, 16)
    v.quantize_mx(T.xkc[:, :], T.xks[:, :], T.xkb[:, :]).then_inc(S.q_xk, 1)
    for i in (1, 0, 3, 2):
        quant_wk(i)
    for b in range(4):
        product(b, 0)
    for b in range(4):
        v.wait_ge(S["zero%d" % (b // 2)], 1)
        scan(b, 0, [("sc%d0" % b, 0, AHEAD)])
    product(0, 1)
    v.wait_ge(S.k_zero, 1)
    for b in range(4):
        v.wait_ge(S["rt%d0" % b], 1)
    v.quantize_mx(T.kca[:, :], T.ksa[:, :], T.kt[:, :]).then_inc(S.q_ahead, 1)
    product(1, 1)
    scan(0, 1, [("sc01", AHEAD, KC)])
    scan(1, 1, [("sc11", AHEAD, KC)])
    product(2, 1)
    product(3, 1)
    scan(2, 1, [("sc21", AHEAD, KC)])
    scan(3, 1, [("sc31", AHEAD, MID), ("sc_end", MID, KC)])
    v.wait_ge(S.q_ahead, 1)
    scaled(3, MID, KC, v, "sc_end", "rt_end")
    v.wait_ge(S.rt_end, 1)
    for b in range(4):
        v.wait_ge(S["rt%d1" % b], 1)
    v.quantize_mx(kc[:, :], ks[:, :], T.kt[:, :]).then_inc(S.q_k, 1)
    v.wait_ge(S.l_xq, 16)
    v.quantize_mx(T.xqc[:, :], T.xqs[:, :], T.xqb[:, :]).then_inc(S.q_xq, 1)

    far_engines = 0
    for ready, piece, src, sem in ((S.q_ahead, first, (T.kca, T.ksa), S.ahead_in), (S.q_k, rest, (kc, ks), S.rest_in)):
        g.wait_ge(ready, 1)
        for k in range(2):
            moves = []
            for f, d in enumerate(far):
                port = via[d][k]
                rid, pid = topo.addr(port, core)
                m = sum(engines(topo.mask(core, port))[1 - f::2])
                moves.append(RemoteDMATransfer(dst_ids=[DstId(rid=rid, pnc=pid)], dma_engine_mask=m, remote_sem=sem,
                                               src=piece(src[0], src[1], k), dst=piece(kc, ks, k)))
                far_engines += count(m)
            g.remote_dma_fused(moves, local_sem=S.sent_far)
    rid, pid = topo.addr(peer, core)
    m = topo.mask(core, peer)
    for piece in (codes(kc, 0, KC), ks[:, 0:KC]):
        g.remote_dma(out_ap=piece, in_ap=piece, remote_sem=S["arr%d" % r], local_sem=S.sent_peer,
                     pid=pid, routing_id=rid, dma_engine_mask=m)
    g.wait_ge(S.sent_far, far_engines)
    g.wait_ge(S.sent_peer, 2 * count(m))

    t.wait_ge(S.q_k, 1)
    t.wait_ge(S.q_xq, 1)
    s.wait_ge(S.sent_far, far_engines)
    for n, j in enumerate(order):
        banks, at = (T.yp, 1024 * n) if n < 2 else (T.z, 1024 * (n - 2))
        left, right = slice(NC * j, NC * j + CUT), slice(NC * j + CUT, NC * j + NC)
        if n == 1:
            t.wait_ge(S["arr%d" % j], 2 * count(topo.mask(peer, core)))
        if n > 1:
            ports = routes(T.cores[j], T, topo)[1][core]
            t.wait_ge(S["arr%d" % j], 2 * sum(count(topo.mask(q, core)) for q in ports))
        for sem, bank, lo, hi in (("bl", at, 0, CUT), ("br", at + 512, CUT, NC)):
            t.matmul_mx(banks[:, bank:bank + hi - lo], T["kc%d" % j][:, 0:KC], T["ks%d" % j][:, 0:KC],
                        T.xqc[:, lo:hi], T.xqs[:, lo:hi], True, True).then_inc(S["%s%d" % (sem, n)], 1)
        v.wait_ge(S["bl%d" % n], 1)
        v.tensor_copy(T.yb[:, left], banks[:, at:at + CUT]).then_inc(S["cl%d" % n], 1)
        a.wait_ge(S["br%d" % n], 1)
        a.activation(T.yb[:, right], banks[:, at + 512:at + 512 + NC - CUT], copy).then_inc(S["cr%d" % n], 1)
        s.wait_ge(S["cl%d" % n], 1)
        if n < N - 1:
            s.wait_ge(S["cr%d" % n], 1)
            s.dma_start(T.y[:, NC * j:NC * j + NC], T.yb[:, NC * j:NC * j + NC]).then_inc(S["st%d" % n], 16)
        else:
            s.dma_start(T.y[:, left], T.yb[:, left]).then_inc(S["st%d" % n], 16)
            a.wait_ge(S["cr%d" % n], 1)
            a.dma_start(T.y[:, right], T.yb[:, right]).then_inc(S.st_last, 16)
    for n in range(N):
        s.wait_ge(S["st%d" % n], 16)
    a.wait_ge(S.st_last, 16)
